import numpy as np
import ml_dtypes


def mxq(x, axis, fmt="e4m3"):
    dtype, down = {"e4m3": (ml_dtypes.float8_e4m3fn, 7), "e5m2": (ml_dtypes.float8_e5m2, 14)}[fmt]
    v = np.moveaxis(np.asarray(x, np.float32).astype(ml_dtypes.bfloat16).astype(np.float64), axis, -1)
    blocks = v.reshape(v.shape[:-1] + (-1, 32))
    amax = np.abs(blocks).max(-1, keepdims=True)
    byte = np.maximum(np.where(amax > 0, np.frexp(amax)[1] - 1 + 127, 0) - down, 1)
    scale = np.exp2(byte - 127.0)
    codes = (blocks / scale).astype(np.float32).astype(dtype).astype(np.float64)
    return np.moveaxis((codes * scale).reshape(v.shape), -1, axis)


WIDE = False


def mx_kscale(k):
    if not WIDE:
        return np.ones(k)
    levels = np.array([10, -10, 5, -5, 0])
    if k % 512:
        return np.exp2(np.random.permutation(np.resize(levels, k // 32))).repeat(32)
    a = np.empty((k // 512, 16))
    for p in range(k // 512):
        a[p, :8] = np.random.permutation(np.resize(levels, 8))
        for g in range(8):
            far = levels[np.abs(levels - a[p, g]) >= 10]
            a[p, g + 8] = far[np.random.randint(len(far))]
    return np.exp2(a.ravel()).repeat(32)


def f64(x):
    return np.asarray(x).astype(np.float64)


def striped(idx):
    return np.tile(idx.reshape(-1, 16).T, (8, 1)).astype(np.uint16)


def unstriped(offs):
    return offs[:16].T.reshape(-1).astype(np.int64)


E2M1 = np.array([0.0, 0.5, 1.0, 1.5, 2.0, 3.0, 4.0, 6.0, -0.0, -0.5, -1.0, -1.5, -2.0, -3.0, -4.0, -6.0])


def pack_weight(w, fmt):
    k, n = w.shape
    w = f64(np.asarray(w, np.float32).astype(ml_dtypes.bfloat16)).reshape(k // 32, 32, n)
    amax = np.abs(w).max(1)
    if fmt == "e4m3":
        byte = np.frexp(amax)[1] - 1 + 127 - 7
    else:
        mant, ex = np.frexp(amax / 6.0)
        byte = np.where(mant > 0.5, ex, ex - 1) + 127
    byte = np.clip(np.where(amax > 0, byte, 1), 1, 254)
    scaled = (w * np.exp2(127.0 - byte)[:, None, :]).reshape(k, n).astype(np.float32)
    by_word = np.ascontiguousarray(scaled.reshape(k // 512, 128, 4, n).transpose(0, 1, 3, 2))
    if fmt == "e4m3":
        words = by_word.astype(ml_dtypes.float8_e4m3fn).view(np.uint8)
    else:
        c = by_word.astype(ml_dtypes.float4_e2m1fn).view(np.uint8) & 0xF
        words = (c[..., 0::2] | (c[..., 1::2] << 4)).reshape(k // 512, 128, 2 * n)
    return np.ascontiguousarray(words), np.ascontiguousarray(byte.astype(np.uint8).reshape(k // 512, 16, n))


def unpack_weight(words, scales, fmt):
    g, _, n = scales.shape
    words = np.ascontiguousarray(words).reshape(g, 128, n, -1)
    if fmt == "e4m3":
        vals = words.view(ml_dtypes.float8_e4m3fn).astype(np.float64)
    else:
        nib = np.empty((g, 128, n, 4), np.uint8)
        nib[..., 0::2] = words & 0xF
        nib[..., 1::2] = words >> 4
        vals = E2M1[nib]
    vals = vals * np.repeat(np.exp2(scales.astype(np.float64) - 127.0), 8, axis=1)[..., None]
    return vals.transpose(0, 1, 3, 2).reshape(g * 512, n)


def gelu(v):
    return 0.5 * v * (1.0 + np.tanh(np.sqrt(2.0 / np.pi) * (v + 0.044715 * v**3)))


T, S, K, K2, H, N = 4096, 1024, 1024, 512, 1024, 512


def setup_inputs():
    n = np.random.standard_normal
    s = mx_kscale(K)[:, None]
    s2 = mx_kscale(K2)[:, None]
    u = mx_kscale(H)[:, None]
    d = {}
    d["tab_words"], d["tab_scales"] = pack_weight(n((K, T)) * s, "e4m3")
    d["offs"] = striped(np.random.permutation(T)[:S])
    d["xs_words"], d["xs_scales"] = pack_weight(n((K2, S)) * s2, "e4m3")
    d["w1"] = (n((K, H)) / K ** 0.5 / s).astype(np.float32)
    d["b1"] = (0.7 * n(H)).astype(np.float32)
    d["w2"] = (1.2 * n((K2, H)) / K2 ** 0.5 / s2 * u.T).astype(np.float32)
    d["w3"] = (n((K2, N)) / K2 ** 0.5 / s2).astype(np.float32)
    d["b3"] = (0.6 * n(N)).astype(np.float32)
    d["w4_words"], d["w4_scales"] = pack_weight(1.6 * n((H, N)) / H ** 0.5 / u, "e2m1")
    return d


def reference(tab_words, tab_scales, offs, xs_words, xs_scales, w1, b1, w2, w3, b3, w4_words, w4_scales):
    v = unpack_weight(tab_words, tab_scales, "e4m3")[:, unstriped(offs)]
    xs = unpack_weight(xs_words, xs_scales, "e4m3")
    tex = (mxq(f64(w1), 0, "e4m3").T @ v) + f64(b1)[:, None]
    wet = mxq(f64(w2), 0, "e4m3").T @ xs
    h = wet * (1.0 / (1.0 + np.square(tex)))
    y = unpack_weight(w4_words, w4_scales, "e2m1").T @ mxq(h, 0, "e4m3")
    cap = (mxq(f64(w3), 0, "e4m3").T @ xs) + f64(b3)[:, None]
    return np.minimum(y, cap)

@@ -1,0 +1,288 @@
+from contextlib import ExitStack
+
+import concourse.mybir as mybir
+
+T, S, K, K2, H, N = 4096, 1024, 1024, 512, 1024, 512
+FLOPS = 2 * S * (K * H + K2 * H + H * N + K2 * N)
+
+F32 = mybir.dt.float32
+BF16 = mybir.dt.bfloat16
+I32 = mybir.dt.int32
+U32 = mybir.dt.uint32
+U16 = mybir.dt.uint16
+U8 = mybir.dt.uint8
+E4M3 = mybir.dt.float8_e4m3fn_x4
+E2M1 = mybir.dt.float4_e2m1fn_x4
+ACT = mybir.ActivationFunctionType
+ALU = mybir.AluOpType
+
+P = 128
+PACK = 4
+KP = P * PACK
+BANK = 512
+CHUNK = 128
+
+
+def tile_list_runway_friction_scores_kernel(
+    tc, tab_words, tab_scales, offs, xs_words, xs_scales, w1, b1, w2, w3, b3, w4_words, w4_scales, out
+):
+    nc = tc.nc
+    with ExitStack() as ctx:
+        keep = ctx.enter_context(tc.tile_pool(name="keep", bufs=1))
+        ring = ctx.enter_context(tc.tile_pool(name="ring", bufs=3))
+        psum = ctx.enter_context(tc.psum_pool(name="psum", bufs=1))
+
+        offsets = keep.tile([P, S // 16], U16, name="offsets")
+        nc.sync.dma_start(offsets[:], offs)
+
+        tab_plane = keep.tile([P, T], U8, name="tab_plane", align_bytes=64)
+        nc.vector.memset(tab_plane[:].bitcast(I32), 0)
+        xs_plane = keep.tile([P, S], U8, name="xs_plane", align_bytes=64)
+        nc.vector.memset(xs_plane[:].bitcast(I32), 0)
+        w4_plane = keep.tile([P, 2, N], U8, name="w4_plane", align_bytes=64)
+        nc.vector.memset(w4_plane[:].rearrange("p a n -> p (a n)").bitcast(I32), 0)
+        warm = keep.tile([P, 8], F32, name="warm")
+        nc.vector.memset(warm[:], 1.0)
+        warm2 = keep.tile([P, 8], F32, name="warm2")
+        nc.scalar.activation(warm2[:], warm[:], ACT.Abs_reciprocal_sqrt, bias=1.0)
+
+        def load_table(a):
+            words = keep.tile([P, T], U32, name="tab%d" % a, align_bytes=64)
+            nc.sync.dma_start(words[:].bitcast(I32), tab_words[a].rearrange("p t i -> p (t i)").bitcast(I32))
+            return words
+
+        def load_weight(name, w, a, b):
+            raw = keep.tile([P, PACK, BANK], F32, name=name)
+            nc.sync.dma_start(
+                raw[:], w[a * KP : (a + 1) * KP, b * BANK : (b + 1) * BANK].rearrange("(p j) c -> p j c", j=PACK)
+            )
+            return raw
+
+        tab0 = load_table(0)
+        for q in range(4):
+            nc.sync.dma_start(
+                tab_plane[32 * q : 32 * q + 8, :].bitcast(I32), tab_scales[:, 4 * q : 4 * q + 4, :].bitcast(I32)
+            )
+        for q in range(4):
+            nc.gpsimd.dma_start(
+                xs_plane[32 * q : 32 * q + 4, :].bitcast(I32), xs_scales[0, 4 * q : 4 * q + 4, :].bitcast(I32)
+            )
+        for q in range(4):
+            nc.gpsimd.dma_start(
+                w4_plane[32 * q : 32 * q + 4, :, :].bitcast(I32),
+                w4_scales[:, 4 * q : 4 * q + 4, :].rearrange("a r n -> r a n").bitcast(I32),
+            )
+
+        raw = {}
+        raw["w1", 0, 0] = load_weight("w1_00", w1, 0, 0)
+        b1_sb = keep.tile([P, 2, PACK], F32, name="b1_sb")
+        nc.sync.dma_start(b1_sb[:], b1.rearrange("(b p t) -> p b t", b=2, t=PACK))
+        raw["w1", 1, 0] = load_weight("w1_10", w1, 1, 0)
+        tab1 = load_table(1)
+        xs = keep.tile([P, S], U32, name="xs", align_bytes=64)
+        w4 = keep.tile([P, 2, 2 * N], U8, name="w4", align_bytes=64)
+        b3_sb = keep.tile([P, PACK], F32, name="b3_sb")
+        raw["w1", 0, 1] = load_weight("w1_01", w1, 0, 1)
+        raw["w1", 1, 1] = load_weight("w1_11", w1, 1, 1)
+        nc.sync.dma_start(xs[:].bitcast(I32), xs_words[0].rearrange("p c i -> p (c i)").bitcast(I32))
+        raw["w2", 0, 0] = load_weight("w2_00", w2, 0, 0)
+        raw["w2", 0, 1] = load_weight("w2_01", w2, 0, 1)
+        raw["w3", 0, 0] = load_weight("w3_00", w3, 0, 0)
+        with nc.allow_non_contiguous_dma(reason="one bias value for each partition"):
+            nc.sync.dma_start(b3_sb[:], b3.rearrange("(g p) -> p g", p=P))
+        nc.sync.dma_start(w4[:].bitcast(I32), w4_words.rearrange("a p c -> p a c").bitcast(I32))
+
+        wq = {}
+
+        def cast(key, engine, pieces):
+            grouped = ring.tile([P, PACK, P, PACK], BF16, name="grouped", align_bytes=64, bufs=3)
+            if key[0] != "w3":
+                src = raw[key][:].rearrange("p j (m u e) -> p u m j e", u=2, e=2)
+                dst = grouped[:].rearrange("p (u e) m j -> p u m j e", e=2)
+            else:
+                src = raw[key][:].rearrange("p j (u m e) -> p u m j e", u=2, e=2)
+                dst = grouped[:].rearrange("p g m j -> p (g m j)").rearrange("p (u m e j) -> p u m j e", u=2, e=2, j=PACK)
+            if engine == "s":
+                nc.scalar.copy(dst, src)
+            elif engine == "v":
+                nc.vector.tensor_copy(dst, src)
+            else:
+                step = 2 * P // pieces
+                for u in range(2):
+                    for m in range(0, P, step):
+                        nc.gpsimd.tensor_scalar(dst[:, u, m : m + step], src[:, u, m : m + step], 1.0, 0.0, ALU.mult, ALU.add)
+            return grouped
+
+        def quantise(key, grouped):
+            codes = keep.tile([P, BANK], U32, name="%s_%d%d_codes" % key, align_bytes=64)
+            plane = keep.tile([P, BANK], U8, name="%s_%d%d_plane" % key, align_bytes=64)
+            nc.vector.quantize_mx(
+                out=codes[:].bitcast(E4M3), scales=plane[:], in_=grouped[:].rearrange("p t m j -> p (t m j)")
+            )
+            wq[key] = (codes, plane)
+
+        def stationary(key, t):
+            codes, plane = wq[key]
+            cols = slice(t * P, (t + 1) * P)
+            return codes[:, cols].bitcast(E4M3), plane[:, cols]
+
+        v0 = keep.tile([P, S], U32, name="v0", align_bytes=64)
+        nc.vector.tensor_copy(v0[:], tab0[:].indirect(offsets[:]))
+        v_plane = keep.tile([P, S], U8, name="v_plane", align_bytes=64)
+        nc.vector.tensor_copy(v_plane[:], tab_plane[:].indirect(offsets[:]))
+        quantise(("w1", 0, 0), cast(("w1", 0, 0), "s", 1))
+        quantise(("w1", 1, 0), cast(("w1", 1, 0), "s", 1))
+        v1 = keep.tile([P, S], U32, name="v1", align_bytes=64)
+        v = [v0, v1]
+
+        def gather1(half):
+            nc.vector.tensor_copy(
+                v1[:, half * BANK : (half + 1) * BANK], tab1[:].indirect(offsets[:, 32 * half : 32 * half + 32])
+            )
+
+        h_codes = [keep.tile([P, S], U32, name="h_codes%d" % b, align_bytes=64) for b in range(2)]
+        h_plane = [keep.tile([P, S], U8, name="h_plane%d" % b, align_bytes=64) for b in range(2)]
+        cap = keep.tile([P, PACK, S], F32, name="cap")
+
+        def damping(b, j0, n, square_on_vector):
+            damp = ring.tile([P, PACK, n], F32, name="damp", bufs=4)
+            cols = slice(j0, j0 + n)
+            per_bank = BANK // n
+            for t0 in range(0, PACK, per_bank):
+                tex = psum.tile([P, per_bank, n], F32, name="tex", bufs=4)
+                for i in range(per_bank):
+                    for a in range(2):
+                        codes, plane = stationary(("w1", a, b), t0 + i)
+                        nc.tensor.matmul_mx(
+                            out=tex[:, i, :],
+                            lhsT=codes,
+                            lhsT_scale=plane,
+                            rhs=v[a][:, cols].bitcast(E4M3),
+                            rhs_scale=v_plane[4 * a : P, cols],
+                            start=(a == 0),
+                            stop=(a == 1),
+                        )
+                for i in range(per_bank):
+                    t = t0 + i
+                    nc.scalar.activation(damp[:, t, :], tex[:, i, :], ACT.Square, bias=b1_sb[:, b, t : t + 1])
+            pairs = [damp[:, 2 * u : 2 * u + 2, :] for u in range(2)]
+            for pair in pairs:
+                nc.scalar.activation(pair, pair, ACT.Abs_reciprocal_sqrt, bias=1.0)
+            for u, pair in enumerate(pairs):
+                if square_on_vector[u] == "v":
+                    nc.vector.tensor_tensor(pair, pair, pair, ALU.mult)
+                elif square_on_vector[u] == "g":
+                    for i in range(2):
+                        nc.gpsimd.tensor_tensor(pair[:, i, :], pair[:, i, :], pair[:, i, :], ALU.mult)
+                else:
+                    nc.scalar.activation(pair, pair, ACT.Square)
+            return damp
+
+        def damped(b, j0, n, damp, off):
+            h = ring.tile([P, n, PACK], BF16, name="h", align_bytes=64, bufs=3)
+            for c in range(n // CHUNK):
+                cols = slice(j0 + c * CHUNK, j0 + (c + 1) * CHUNK)
+                wet = psum.tile([P, PACK, CHUNK], F32, name="wet", bufs=2)
+                for t in range(PACK):
+                    codes, plane = stationary(("w2", 0, b), t)
+                    nc.tensor.matmul_mx(
+                        out=wet[:, t, :],
+                        lhsT=codes,
+                        lhsT_scale=plane,
+                        rhs=xs[:, cols].bitcast(E4M3),
+                        rhs_scale=xs_plane[:, cols],
+                        start=True,
+                        stop=True,
+                    )
+                nc.vector.tensor_tensor(
+                    h[:, c * CHUNK : (c + 1) * CHUNK, :].rearrange("p (c e) t -> p c t e", e=2),
+                    wet[:].rearrange("p t (c e) -> p c t e", e=2),
+                    damp[:, :, off + c * CHUNK : off + (c + 1) * CHUNK].rearrange("p t (c e) -> p c t e", e=2),
+                    ALU.mult,
+                )
+            return h
+
+        def quantise_h(b, j0, n, h):
+            cols = slice(j0, j0 + n)
+            nc.vector.quantize_mx(
+                out=h_codes[b][:, cols].bitcast(E4M3), scales=h_plane[b][:, cols], in_=h[:].rearrange("p c t -> p (c t)")
+            )
+
+        def scores(j0):
+            cols = slice(j0, j0 + CHUNK)
+            y = psum.tile([P, PACK, CHUNK], F32, name="y", bufs=2)
+            for g in range(PACK):
+                for a in range(2):
+                    nc.tensor.matmul_mx(
+                        out=y[:, g, :],
+                        lhsT=w4[:, a, 2 * g * P : 2 * (g + 1) * P].bitcast(E2M1),
+                        lhsT_scale=w4_plane[:, a, g * P : (g + 1) * P],
+                        rhs=h_codes[a][:, cols].bitcast(E4M3),
+                        rhs_scale=h_plane[a][:, cols],
+                        start=(a == 0),
+                        stop=(a == 1),
+                    )
+            res = ring.tile([P, PACK, CHUNK], F32, name="res", bufs=4)
+            nc.vector.tensor_tensor(res[:], y[:], cap[:, :, cols], ALU.min)
+            nc.sync.dma_start(out[:, cols].rearrange("(g p) j -> p g j", p=P), res[:])
+
+        def caps(half, on_scalar):
+            cols = slice(half * BANK, (half + 1) * BANK)
+            for g in range(PACK):
+                acc = psum.tile([P, BANK], F32, name="y", bufs=2)
+                codes, plane = stationary(("w3", 0, 0), g)
+                nc.tensor.matmul_mx(
+                    out=acc[:],
+                    lhsT=codes,
+                    lhsT_scale=plane,
+                    rhs=xs[:, cols].bitcast(E4M3),
+                    rhs_scale=xs_plane[:, cols],
+                    start=True,
+                    stop=True,
+                )
+                if on_scalar[g]:
+                    nc.scalar.activation(cap[:, g, cols], acc[:], ACT.Identity, bias=b3_sb[:, g : g + 1])
+                else:
+                    nc.vector.tensor_scalar(cap[:, g, cols], acc[:], b3_sb[:, g : g + 1], None, ALU.add)
+
+        gather1(0)
+        d00 = damping(0, 0, 512, "ss")
+        quantise(("w1", 0, 1), cast(("w1", 0, 1), "v", 4))
+        quantise(("w1", 1, 1), cast(("w1", 1, 1), "v", 4))
+        gather1(1)
+        d10 = damping(1, 0, 512, "ss")
+        quantise(("w2", 0, 0), cast(("w2", 0, 0), "v", 4))
+        g = cast(("w2", 0, 1), "v", 4)
+        h = damped(0, 0, 512, d00, 0)
+        quantise(("w2", 0, 1), g)
+        d02 = damping(0, 512, 256, "ss")
+        g = cast(("w3", 0, 0), "v", 4)
+        quantise_h(0, 0, 512, h)
+        quantise(("w3", 0, 0), g)
+        caps(0, (0,0,0,0))
+        d12 = damping(1, 512, 256, "ss")
+        ha = damped(1, 0, 256, d10, 0)
+        hb = damped(1, 256, 256, d10, 256)
+        quantise_h(1, 0, 256, ha)
+        quantise_h(1, 256, 256, hb)
+        d03 = damping(0, 768, 256, "ss")
+        h = damped(0, 512, 256, d02, 0)
+        scores(0)
+        scores(128)
+        quantise_h(0, 512, 256, h)
+        scores(256)
+        scores(384)
+        d13 = damping(1, 768, 256, "ss")
+        caps(1, (1,0,0,0))
+        h = damped(1, 512, 256, d12, 0)
+        hb = damped(0, 768, 256, d03, 0)
+        quantise_h(1, 512, 256, h)
+        quantise_h(0, 768, 256, hb)
+        scores(512)
+        scores(640)
+        hb = damped(1, 768, 128, d13, 0)
+        hc = damped(1, 896, 128, d13, 128)
+        quantise_h(1, 768, 128, hb)
+        quantise_h(1, 896, 128, hc)
+        scores(768)
+        scores(896)

@@ -58,41 +58,45 @@ def tile_list_runway_friction_scores_kernel(
             )
             return raw
 
+        raw = {}
+        b1_sb = keep.tile([P, 2, PACK], F32, name="b1_sb")
+        xs = keep.tile([P, S], U32, name="xs", align_bytes=64)
+        w4 = keep.tile([P, 2, 2 * N], U8, name="w4", align_bytes=64)
+        b3_sb = keep.tile([P, PACK], F32, name="b3_sb")
         tab0 = load_table(0)
         for q in range(4):
             nc.sync.dma_start(
-                tab_plane[32 * q : 32 * q + 8, :].bitcast(I32), tab_scales[:, 4 * q : 4 * q + 4, :].bitcast(I32)
+                tab_plane[32 * q + 0 : 32 * q + 4, :].bitcast(I32), tab_scales[0, 4 * q : 4 * q + 4, :].bitcast(I32)
             )
+        raw["w1", 0, 0] = load_weight("w1_00", w1, 0, 0)
+        for q in range(4):
+            nc.sync.dma_start(
+                tab_plane[32 * q + 4 : 32 * q + 8, :].bitcast(I32), tab_scales[1, 4 * q : 4 * q + 4, :].bitcast(I32)
+            )
+        raw["w1", 1, 0] = load_weight("w1_10", w1, 1, 0)
+        nc.sync.dma_start(b1_sb[:], b1.rearrange("(b p t) -> p b t", b=2, t=PACK))
+        tab1 = load_table(1)
         for q in range(4):
             nc.gpsimd.dma_start(
                 xs_plane[32 * q : 32 * q + 4, :].bitcast(I32), xs_scales[0, 4 * q : 4 * q + 4, :].bitcast(I32)
             )
+        raw["w1", 0, 1] = load_weight("w1_01", w1, 0, 1)
+        raw["w1", 1, 1] = load_weight("w1_11", w1, 1, 1)
+        nc.sync.dma_start(xs[:].bitcast(I32), xs_words[0].rearrange("p c i -> p (c i)").bitcast(I32))
+        raw["w2", 0, 0] = load_weight("w2_00", w2, 0, 0)
         for q in range(4):
             nc.gpsimd.dma_start(
                 w4_plane[32 * q : 32 * q + 4, :, :].bitcast(I32),
                 w4_scales[:, 4 * q : 4 * q + 4, :].rearrange("a r n -> r a n").bitcast(I32),
             )
-
-        raw = {}
-        raw["w1", 0, 0] = load_weight("w1_00", w1, 0, 0)
-        b1_sb = keep.tile([P, 2, PACK], F32, name="b1_sb")
-        nc.sync.dma_start(b1_sb[:], b1.rearrange("(b p t) -> p b t", b=2, t=PACK))
-        raw["w1", 1, 0] = load_weight("w1_10", w1, 1, 0)
-        tab1 = load_table(1)
-        xs = keep.tile([P, S], U32, name="xs", align_bytes=64)
-        w4 = keep.tile([P, 2, 2 * N], U8, name="w4", align_bytes=64)
-        b3_sb = keep.tile([P, PACK], F32, name="b3_sb")
-        raw["w1", 0, 1] = load_weight("w1_01", w1, 0, 1)
-        raw["w1", 1, 1] = load_weight("w1_11", w1, 1, 1)
-        nc.sync.dma_start(xs[:].bitcast(I32), xs_words[0].rearrange("p c i -> p (c i)").bitcast(I32))
-        raw["w2", 0, 0] = load_weight("w2_00", w2, 0, 0)
-        raw["w2", 0, 1] = load_weight("w2_01", w2, 0, 1)
-        raw["w3", 0, 0] = load_weight("w3_00", w3, 0, 0)
         with nc.allow_non_contiguous_dma(reason="one bias value for each partition"):
             nc.sync.dma_start(b3_sb[:], b3.rearrange("(g p) -> p g", p=P))
+        raw["w3", 0, 0] = load_weight("w3_00", w3, 0, 0)
+        raw["w2", 0, 1] = load_weight("w2_01", w2, 0, 1)
         nc.sync.dma_start(w4[:].bitcast(I32), w4_words.rearrange("a p c -> p a c").bitcast(I32))
 
         wq = {}
+        held = {}
 
         def cast(key, engine, pieces):
             grouped = ring.tile([P, PACK, P, PACK], BF16, name="grouped", align_bytes=64, bufs=3)
@@ -106,6 +110,9 @@ def tile_list_runway_friction_scores_kernel(
                 nc.scalar.copy(dst, src)
             elif engine == "v":
                 nc.vector.tensor_copy(dst, src)
+            elif engine == "h":
+                for u in range(2):
+                    nc.vector.tensor_copy(dst[:, u], src[:, u])
             else:
                 step = 2 * P // pieces
                 for u in range(2):
@@ -113,12 +120,17 @@ def tile_list_runway_friction_scores_kernel(
                         nc.gpsimd.tensor_scalar(dst[:, u, m : m + step], src[:, u, m : m + step], 1.0, 0.0, ALU.mult, ALU.add)
             return grouped
 
-        def quantise(key, grouped):
+        def quantise(key, grouped, parts=1):
             codes = keep.tile([P, BANK], U32, name="%s_%d%d_codes" % key, align_bytes=64)
             plane = keep.tile([P, BANK], U8, name="%s_%d%d_plane" % key, align_bytes=64)
-            nc.vector.quantize_mx(
-                out=codes[:].bitcast(E4M3), scales=plane[:], in_=grouped[:].rearrange("p t m j -> p (t m j)")
-            )
+            flat = grouped[:].rearrange("p t m j -> p (t m j)")
+            step = BANK // parts
+            for c in range(0, BANK, step):
+                nc.vector.quantize_mx(
+                    out=codes[:, c : c + step].bitcast(E4M3),
+                    scales=plane[:, c : c + step],
+                    in_=flat[:, PACK * c : PACK * (c + step)],
+                )
             wq[key] = (codes, plane)
 
         def stationary(key, t):
@@ -127,24 +139,25 @@ def tile_list_runway_friction_scores_kernel(
             return codes[:, cols].bitcast(E4M3), plane[:, cols]
 
         v0 = keep.tile([P, S], U32, name="v0", align_bytes=64)
-        nc.vector.tensor_copy(v0[:], tab0[:].indirect(offsets[:]))
         v_plane = keep.tile([P, S], U8, name="v_plane", align_bytes=64)
-        nc.vector.tensor_copy(v_plane[:], tab_plane[:].indirect(offsets[:]))
-        quantise(("w1", 0, 0), cast(("w1", 0, 0), "s", 1))
-        quantise(("w1", 1, 0), cast(("w1", 1, 0), "s", 1))
-        v1 = keep.tile([P, S], U32, name="v1", align_bytes=64)
-        v = [v0, v1]
+        v1 = [keep.tile([P, BANK], U32, name="v1_%d" % i, align_bytes=64) for i in range(2)]
+
+        def gather0():
+            nc.vector.tensor_copy(v0[:], tab0[:].indirect(offsets[:]))
+
+        def gather_scales():
+            nc.vector.tensor_copy(v_plane[:], tab_plane[:].indirect(offsets[:]))
 
         def gather1(half):
             nc.vector.tensor_copy(
-                v1[:, half * BANK : (half + 1) * BANK], tab1[:].indirect(offsets[:, 32 * half : 32 * half + 32])
+                v1[half][:], tab1[:].indirect(offsets[:, 32 * half : 32 * half + 32])
             )
 
         h_codes = [keep.tile([P, S], U32, name="h_codes%d" % b, align_bytes=64) for b in range(2)]
         h_plane = [keep.tile([P, S], U8, name="h_plane%d" % b, align_bytes=64) for b in range(2)]
-        cap = keep.tile([P, PACK, S], F32, name="cap")
+        cap = [keep.tile([P, PACK, BANK], F32, name="cap%d" % i) for i in range(2)]
 
-        def damping(b, j0, n, square_on_vector):
+        def damping(b, j0, n, square_on_vector, by_tokens=False):
             damp = ring.tile([P, PACK, n], F32, name="damp", bufs=4)
             cols = slice(j0, j0 + n)
             per_bank = BANK // n
@@ -157,7 +170,7 @@ def tile_list_runway_friction_scores_kernel(
                             out=tex[:, i, :],
                             lhsT=codes,
                             lhsT_scale=plane,
-                            rhs=v[a][:, cols].bitcast(E4M3),
+                            rhs=(v0[:, cols] if a == 0 else v1[j0 // BANK][:, j0 % BANK : j0 % BANK + n]).bitcast(E4M3),
                             rhs_scale=v_plane[4 * a : P, cols],
                             start=(a == 0),
                             stop=(a == 1),
@@ -166,20 +179,28 @@ def tile_list_runway_friction_scores_kernel(
                     t = t0 + i
                     nc.scalar.activation(damp[:, t, :], tex[:, i, :], ACT.Square, bias=b1_sb[:, b, t : t + 1])
             pairs = [damp[:, 2 * u : 2 * u + 2, :] for u in range(2)]
+            if by_tokens:
+                pairs = [damp[:, :, u * n // 2 : (u + 1) * n // 2] for u in range(2)]
             for pair in pairs:
                 nc.scalar.activation(pair, pair, ACT.Abs_reciprocal_sqrt, bias=1.0)
+            squared(pairs, square_on_vector)
+            held[b, j0] = pairs
+            return damp
+
+        def squared(pairs, square_on_vector):
             for u, pair in enumerate(pairs):
+                if square_on_vector[u] == "-":
+                    continue
                 if square_on_vector[u] == "v":
                     nc.vector.tensor_tensor(pair, pair, pair, ALU.mult)
                 elif square_on_vector[u] == "g":
-                    for i in range(2):
+                    for i in range(pair.shape[1]):
                         nc.gpsimd.tensor_tensor(pair[:, i, :], pair[:, i, :], pair[:, i, :], ALU.mult)
                 else:
                     nc.scalar.activation(pair, pair, ACT.Square)
-            return damp
 
         def damped(b, j0, n, damp, off):
-            h = ring.tile([P, n, PACK], BF16, name="h", align_bytes=64, bufs=3)
+            h = ring.tile([P, n, PACK], BF16, name="h", align_bytes=64, bufs=4)
             for c in range(n // CHUNK):
                 cols = slice(j0 + c * CHUNK, j0 + (c + 1) * CHUNK)
                 wet = psum.tile([P, PACK, CHUNK], F32, name="wet", bufs=2)
@@ -223,8 +244,25 @@ def tile_list_runway_friction_scores_kernel(
                         stop=(a == 1),
                     )
             res = ring.tile([P, PACK, CHUNK], F32, name="res", bufs=4)
-            nc.vector.tensor_tensor(res[:], y[:], cap[:, :, cols], ALU.min)
+            nc.vector.tensor_tensor(res[:], y[:], cap[j0 // BANK][:, :, j0 % BANK : j0 % BANK + CHUNK], ALU.min)
             nc.sync.dma_start(out[:, cols].rearrange("(g p) j -> p g j", p=P), res[:])
+
+        def scores_wide(half, g):
+            cols = slice(half * BANK, (half + 1) * BANK)
+            y = psum.tile([P, BANK], F32, name="y", bufs=2)
+            for a in range(2):
+                nc.tensor.matmul_mx(
+                    out=y[:],
+                    lhsT=w4[:, a, 2 * g * P : 2 * (g + 1) * P].bitcast(E2M1),
+                    lhsT_scale=w4_plane[:, a, g * P : (g + 1) * P],
+                    rhs=h_codes[a][:, cols].bitcast(E4M3),
+                    rhs_scale=h_plane[a][:, cols],
+                    start=(a == 0),
+                    stop=(a == 1),
+                )
+            res = ring.tile([P, BANK], F32, name="res", bufs=4)
+            nc.vector.tensor_tensor(res[:], y[:], cap[half][:, g, :], ALU.min)
+            nc.sync.dma_start(out[g * P : (g + 1) * P, cols], res[:])
 
         def caps(half, on_scalar):
             cols = slice(half * BANK, (half + 1) * BANK)
@@ -241,48 +279,52 @@ def tile_list_runway_friction_scores_kernel(
                     stop=True,
                 )
                 if on_scalar[g]:
-                    nc.scalar.activation(cap[:, g, cols], acc[:], ACT.Identity, bias=b3_sb[:, g : g + 1])
+                    nc.scalar.activation(cap[half][:, g, :], acc[:], ACT.Identity, bias=b3_sb[:, g : g + 1])
                 else:
-                    nc.vector.tensor_scalar(cap[:, g, cols], acc[:], b3_sb[:, g : g + 1], None, ALU.add)
+                    nc.vector.tensor_scalar(cap[half][:, g, :], acc[:], b3_sb[:, g : g + 1], None, ALU.add)
 
+        gather0()
+        gather_scales()
+        quantise(("w1", 0, 0), cast(("w1", 0, 0), "s", 4))
+        quantise(("w1", 1, 0), cast(("w1", 1, 0), "s", 4))
         gather1(0)
-        d00 = damping(0, 0, 512, "ss")
-        quantise(("w1", 0, 1), cast(("w1", 0, 1), "v", 4))
-        quantise(("w1", 1, 1), cast(("w1", 1, 1), "v", 4))
-        gather1(1)
+        d00 = damping(0, 0, 512, "--")
+        quantise(("w1", 0, 1), cast(("w1", 0, 1), "h", 4), 2)
+        quantise(("w1", 1, 1), cast(("w1", 1, 1), "h", 4), 2)
         d10 = damping(1, 0, 512, "ss")
-        quantise(("w2", 0, 0), cast(("w2", 0, 0), "v", 4))
-        g = cast(("w2", 0, 1), "v", 4)
+        gather1(1)
+        quantise(("w2", 0, 0), cast(("w2", 0, 0), "v", 4), 2)
+        squared(held[0, 0], "vv")
+        quantise(("w3", 0, 0), cast(("w3", 0, 0), "v", 4), 2)
+        quantise(("w2", 0, 1), cast(("w2", 0, 1), "v", 4), 2)
+        squared(held[1, 0], "--")
         h = damped(0, 0, 512, d00, 0)
-        quantise(("w2", 0, 1), g)
+        caps(0, (1,0,0,0))
         d02 = damping(0, 512, 256, "ss")
-        g = cast(("w3", 0, 0), "v", 4)
-        quantise_h(0, 0, 512, h)
-        quantise(("w3", 0, 0), g)
-        caps(0, (0,0,0,0))
         d12 = damping(1, 512, 256, "ss")
-        ha = damped(1, 0, 256, d10, 0)
-        hb = damped(1, 256, 256, d10, 256)
-        quantise_h(1, 0, 256, ha)
-        quantise_h(1, 256, 256, hb)
+        ha = damped(1, 0, 512, d10, 0)
+        quantise_h(0, 0, 512, h)
+        caps(1, (1,1,1,1))
         d03 = damping(0, 768, 256, "ss")
         h = damped(0, 512, 256, d02, 0)
-        scores(0)
-        scores(128)
+        quantise_h(1, 0, 512, ha)
+        scores_wide(0, 0)
+        scores_wide(0, 1)
         quantise_h(0, 512, 256, h)
-        scores(256)
-        scores(384)
-        d13 = damping(1, 768, 256, "ss")
-        caps(1, (1,0,0,0))
+        scores_wide(0, 2)
+        scores_wide(0, 3)
+        d13 = damping(1, 768, 256, "ss", True)
         h = damped(1, 512, 256, d12, 0)
-        hb = damped(0, 768, 256, d03, 0)
+        hb = damped(0, 768, 128, d03, 0)
         quantise_h(1, 512, 256, h)
-        quantise_h(0, 768, 256, hb)
+        hc = damped(0, 896, 128, d03, 128)
+        quantise_h(0, 768, 128, hb)
         scores(512)
+        quantise_h(0, 896, 128, hc)
         scores(640)
         hb = damped(1, 768, 128, d13, 0)
-        hc = damped(1, 896, 128, d13, 128)
         quantise_h(1, 768, 128, hb)
+        hc = damped(1, 896, 128, d13, 128)
         quantise_h(1, 896, 128, hc)
         scores(768)
         scores(896)

@@ -80,10 +80,10 @@ def tile_list_runway_friction_scores_kernel(
             nc.gpsimd.dma_start(
                 xs_plane[32 * q : 32 * q + 4, :].bitcast(I32), xs_scales[0, 4 * q : 4 * q + 4, :].bitcast(I32)
             )
-        raw["w1", 0, 1] = load_weight("w1_01", w1, 0, 1)
-        raw["w1", 1, 1] = load_weight("w1_11", w1, 1, 1)
-        nc.sync.dma_start(xs[:].bitcast(I32), xs_words[0].rearrange("p c i -> p (c i)").bitcast(I32))
         raw["w2", 0, 0] = load_weight("w2_00", w2, 0, 0)
+        raw["w1", 0, 1] = load_weight("w1_01", w1, 0, 1)
+        nc.sync.dma_start(xs[:].bitcast(I32), xs_words[0].rearrange("p c i -> p (c i)").bitcast(I32))
+        raw["w1", 1, 1] = load_weight("w1_11", w1, 1, 1)
         for q in range(4):
             nc.gpsimd.dma_start(
                 w4_plane[32 * q : 32 * q + 4, :, :].bitcast(I32),
@@ -264,24 +264,63 @@ def tile_list_runway_friction_scores_kernel(
             nc.vector.tensor_tensor(res[:], y[:], cap[half][:, g, :], ALU.min)
             nc.sync.dma_start(out[g * P : (g + 1) * P, cols], res[:])
 
-        def caps(half, on_scalar):
-            cols = slice(half * BANK, (half + 1) * BANK)
+        def open_scores(j0):
+            cols = slice(j0, j0 + CHUNK)
+            banks = []
             for g in range(PACK):
-                acc = psum.tile([P, BANK], F32, name="y", bufs=2)
-                codes, plane = stationary(("w3", 0, 0), g)
-                nc.tensor.matmul_mx(
-                    out=acc[:],
-                    lhsT=codes,
-                    lhsT_scale=plane,
-                    rhs=xs[:, cols].bitcast(E4M3),
-                    rhs_scale=xs_plane[:, cols],
-                    start=True,
-                    stop=True,
+                y = psum.tile([P, CHUNK], F32, name="tex", bufs=4)
+                score_pass(y, g, 0, cols)
+                banks.append(y)
+            return banks
+
+        def score_pass(y, g, a, cols):
+            nc.tensor.matmul_mx(
+                out=y[:],
+                lhsT=w4[:, a, 2 * g * P : 2 * (g + 1) * P].bitcast(E2M1),
+                lhsT_scale=w4_plane[:, a, g * P : (g + 1) * P],
+                rhs=h_codes[a][:, cols].bitcast(E4M3),
+                rhs_scale=h_plane[a][:, cols],
+                start=(a == 0),
+                stop=(a == 1),
+            )
+
+        def close_scores(j0, banks):
+            cols = slice(j0, j0 + CHUNK)
+            for g in range(PACK):
+                score_pass(banks[g], g, 1, cols)
+            for u, queue in enumerate((nc.sync, nc.scalar)):
+                res = ring.tile([P, 2, CHUNK], F32, name="res", bufs=4)
+                for i in range(2):
+                    g = 2 * u + i
+                    nc.vector.tensor_tensor(
+                        res[:, i, :], banks[g][:], cap[j0 // BANK][:, g, j0 % BANK : j0 % BANK + CHUNK], ALU.min
+                    )
+                queue.dma_start(
+                    out[2 * u * P : 2 * (u + 1) * P, cols].rearrange("(g p) j -> p g j", p=P), res[:]
                 )
-                if on_scalar[g]:
-                    nc.scalar.activation(cap[half][:, g, :], acc[:], ACT.Identity, bias=b3_sb[:, g : g + 1])
-                else:
-                    nc.vector.tensor_scalar(cap[half][:, g, :], acc[:], b3_sb[:, g : g + 1], None, ALU.add)
+
+        def caps(half, on_scalar, j0=0, n=BANK):
+            cols = slice(half * BANK + j0, half * BANK + j0 + n)
+            per_bank = BANK // n
+            for g0 in range(0, PACK, per_bank):
+                acc = psum.tile([P, per_bank, n], F32, name="tex" if on_scalar[g0] else "y", bufs=4 if on_scalar[g0] else 2)
+                for i in range(per_bank):
+                    codes, plane = stationary(("w3", 0, 0), g0 + i)
+                    nc.tensor.matmul_mx(
+                        out=acc[:, i, :],
+                        lhsT=codes,
+                        lhsT_scale=plane,
+                        rhs=xs[:, cols].bitcast(E4M3),
+                        rhs_scale=xs_plane[:, cols],
+                        start=True,
+                        stop=True,
+                    )
+                for i in range(per_bank):
+                    g = g0 + i
+                    if on_scalar[g]:
+                        nc.scalar.activation(cap[half][:, g, j0 : j0 + n], acc[:, i, :], ACT.Identity, bias=b3_sb[:, g : g + 1])
+                    else:
+                        nc.vector.tensor_scalar(cap[half][:, g, j0 : j0 + n], acc[:, i, :], b3_sb[:, g : g + 1], None, ALU.add)
 
         gather0()
         gather_scales()
@@ -289,42 +328,39 @@ def tile_list_runway_friction_scores_kernel(
         quantise(("w1", 1, 0), cast(("w1", 1, 0), "s", 4))
         gather1(0)
         d00 = damping(0, 0, 512, "--")
-        quantise(("w1", 0, 1), cast(("w1", 0, 1), "h", 4), 2)
-        quantise(("w1", 1, 1), cast(("w1", 1, 1), "h", 4), 2)
-        d10 = damping(1, 0, 512, "ss")
         gather1(1)
-        quantise(("w2", 0, 0), cast(("w2", 0, 0), "v", 4), 2)
+        d01 = damping(0, 512, 512, "ss")
+        quantise(("w2", 0, 0), cast(("w2", 0, 0), "v", 4), 1)
+        quantise(("w1", 0, 1), cast(("w1", 0, 1), "v", 4), 1)
+        quantise(("w1", 1, 1), cast(("w1", 1, 1), "v", 4), 1)
+        d10 = damping(1, 0, 512, "ss")
         squared(held[0, 0], "vv")
-        quantise(("w3", 0, 0), cast(("w3", 0, 0), "v", 4), 2)
-        quantise(("w2", 0, 1), cast(("w2", 0, 1), "v", 4), 2)
-        squared(held[1, 0], "--")
         h = damped(0, 0, 512, d00, 0)
-        caps(0, (1,0,0,0))
-        d02 = damping(0, 512, 256, "ss")
+        squared(held[0, 512], "--")
+        quantise_h(0, 0, 512, h)
+        quantise(("w3", 0, 0), cast(("w3", 0, 0), "v", 4), 1)
+        quantise(("w2", 0, 1), cast(("w2", 0, 1), "v", 4), 1)
+        hb = damped(0, 512, 512, d01, 0)
+        quantise_h(0, 512, 512, hb)
         d12 = damping(1, 512, 256, "ss")
         ha = damped(1, 0, 512, d10, 0)
-        quantise_h(0, 0, 512, h)
-        caps(1, (1,1,1,1))
-        d03 = damping(0, 768, 256, "ss")
-        h = damped(0, 512, 256, d02, 0)
+        caps(0, (1,0,1,0))
         quantise_h(1, 0, 512, ha)
+        caps(1, (1,1,1,1), 0, 256)
+        d13 = damping(1, 768, 256, "ss", True)
+        caps(1, (1,1,1,1), 256, 256)
         scores_wide(0, 0)
         scores_wide(0, 1)
-        quantise_h(0, 512, 256, h)
-        scores_wide(0, 2)
-        scores_wide(0, 3)
-        d13 = damping(1, 768, 256, "ss", True)
         h = damped(1, 512, 256, d12, 0)
-        hb = damped(0, 768, 128, d03, 0)
+        scores_wide(0, 2)
         quantise_h(1, 512, 256, h)
-        hc = damped(0, 896, 128, d03, 128)
-        quantise_h(0, 768, 128, hb)
+        scores_wide(0, 3)
         scores(512)
-        quantise_h(0, 896, 128, hc)
-        scores(640)
+        last = open_scores(896)
         hb = damped(1, 768, 128, d13, 0)
+        scores(640)
         quantise_h(1, 768, 128, hb)
         hc = damped(1, 896, 128, d13, 128)
         quantise_h(1, 896, 128, hc)
         scores(768)
-        scores(896)
+        close_scores(896, last)

from contextlib import ExitStack

import concourse.mybir as mybir

T, S, K, K2, H, N = 4096, 1024, 1024, 512, 1024, 512
FLOPS = 2 * S * (K * H + K2 * H + H * N + K2 * N)

F32 = mybir.dt.float32
BF16 = mybir.dt.bfloat16
I32 = mybir.dt.int32
U32 = mybir.dt.uint32
U16 = mybir.dt.uint16
U8 = mybir.dt.uint8
E4M3 = mybir.dt.float8_e4m3fn_x4
E2M1 = mybir.dt.float4_e2m1fn_x4
ACT = mybir.ActivationFunctionType
ALU = mybir.AluOpType

P = 128
PACK = 4
KP = P * PACK
BANK = 512
CHUNK = 128


def tile_list_runway_friction_scores_kernel(
    tc, tab_words, tab_scales, offs, xs_words, xs_scales, w1, b1, w2, w3, b3, w4_words, w4_scales, out
):
    nc = tc.nc
    with ExitStack() as ctx:
        keep = ctx.enter_context(tc.tile_pool(name="keep", bufs=1))
        ring = ctx.enter_context(tc.tile_pool(name="ring", bufs=3))
        psum = ctx.enter_context(tc.psum_pool(name="psum", bufs=1))

        offsets = keep.tile([P, S // 16], U16, name="offsets")
        nc.sync.dma_start(offsets[:], offs)

        tab_plane = keep.tile([P, T], U8, name="tab_plane", align_bytes=64)
        nc.vector.memset(tab_plane[:].bitcast(I32), 0)
        xs_plane = keep.tile([P, S], U8, name="xs_plane", align_bytes=64)
        nc.vector.memset(xs_plane[:].bitcast(I32), 0)
        w4_plane = keep.tile([P, 2, N], U8, name="w4_plane", align_bytes=64)
        nc.vector.memset(w4_plane[:].rearrange("p a n -> p (a n)").bitcast(I32), 0)
        warm = keep.tile([P, 8], F32, name="warm")
        nc.vector.memset(warm[:], 1.0)
        warm2 = keep.tile([P, 8], F32, name="warm2")
        nc.scalar.activation(warm2[:], warm[:], ACT.Abs_reciprocal_sqrt, bias=1.0)

        def load_table(a):
            words = keep.tile([P, T], U32, name="tab%d" % a, align_bytes=64)
            nc.sync.dma_start(words[:].bitcast(I32), tab_words[a].rearrange("p t i -> p (t i)").bitcast(I32))
            return words

        def load_weight(name, w, a, b):
            raw = keep.tile([P, PACK, BANK], F32, name=name)
            nc.sync.dma_start(
                raw[:], w[a * KP : (a + 1) * KP, b * BANK : (b + 1) * BANK].rearrange("(p j) c -> p j c", j=PACK)
            )
            return raw

        raw = {}
        b1_sb = keep.tile([P, 2, PACK], F32, name="b1_sb")
        xs = keep.tile([P, S], U32, name="xs", align_bytes=64)
        w4 = keep.tile([P, 2, 2 * N], U8, name="w4", align_bytes=64)
        b3_sb = keep.tile([P, PACK], F32, name="b3_sb")
        tab0 = load_table(0)
        for q in range(4):
            nc.sync.dma_start(
                tab_plane[32 * q + 0 : 32 * q + 4, :].bitcast(I32), tab_scales[0, 4 * q : 4 * q + 4, :].bitcast(I32)
            )
        raw["w1", 0, 0] = load_weight("w1_00", w1, 0, 0)
        for q in range(4):
            nc.sync.dma_start(
                tab_plane[32 * q + 4 : 32 * q + 8, :].bitcast(I32), tab_scales[1, 4 * q : 4 * q + 4, :].bitcast(I32)
            )
        raw["w1", 1, 0] = load_weight("w1_10", w1, 1, 0)
        nc.sync.dma_start(b1_sb[:], b1.rearrange("(b p t) -> p b t", b=2, t=PACK))
        tab1 = load_table(1)
        for q in range(4):
            nc.gpsimd.dma_start(
                xs_plane[32 * q : 32 * q + 4, :].bitcast(I32), xs_scales[0, 4 * q : 4 * q + 4, :].bitcast(I32)
            )
        raw["w2", 0, 0] = load_weight("w2_00", w2, 0, 0)
        raw["w1", 0, 1] = load_weight("w1_01", w1, 0, 1)
        nc.sync.dma_start(xs[:].bitcast(I32), xs_words[0].rearrange("p c i -> p (c i)").bitcast(I32))
        raw["w1", 1, 1] = load_weight("w1_11", w1, 1, 1)
        for q in range(4):
            nc.gpsimd.dma_start(
                w4_plane[32 * q : 32 * q + 4, :, :].bitcast(I32),
                w4_scales[:, 4 * q : 4 * q + 4, :].rearrange("a r n -> r a n").bitcast(I32),
            )
        with nc.allow_non_contiguous_dma(reason="one bias value for each partition"):
            nc.sync.dma_start(b3_sb[:], b3.rearrange("(g p) -> p g", p=P))
        raw["w3", 0, 0] = load_weight("w3_00", w3, 0, 0)
        raw["w2", 0, 1] = load_weight("w2_01", w2, 0, 1)
        nc.sync.dma_start(w4[:].bitcast(I32), w4_words.rearrange("a p c -> p a c").bitcast(I32))

        wq = {}
        held = {}

        def cast(key, engine, pieces):
            grouped = ring.tile([P, PACK, P, PACK], BF16, name="grouped", align_bytes=64, bufs=3)
            if key[0] != "w3":
                src = raw[key][:].rearrange("p j (m u e) -> p u m j e", u=2, e=2)
                dst = grouped[:].rearrange("p (u e) m j -> p u m j e", e=2)
            else:
                src = raw[key][:].rearrange("p j (u m e) -> p u m j e", u=2, e=2)
                dst = grouped[:].rearrange("p g m j -> p (g m j)").rearrange("p (u m e j) -> p u m j e", u=2, e=2, j=PACK)
            if engine == "s":
                nc.scalar.copy(dst, src)
            elif engine == "v":
                nc.vector.tensor_copy(dst, src)
            elif engine == "h":
                for u in range(2):
                    nc.vector.tensor_copy(dst[:, u], src[:, u])
            else:
                step = 2 * P // pieces
                for u in range(2):
                    for m in range(0, P, step):
                        nc.gpsimd.tensor_scalar(dst[:, u, m : m + step], src[:, u, m : m + step], 1.0, 0.0, ALU.mult, ALU.add)
            return grouped

        def quantise(key, grouped, parts=1):
            codes = keep.tile([P, BANK], U32, name="%s_%d%d_codes" % key, align_bytes=64)
            plane = keep.tile([P, BANK], U8, name="%s_%d%d_plane" % key, align_bytes=64)
            flat = grouped[:].rearrange("p t m j -> p (t m j)")
            step = BANK // parts
            for c in range(0, BANK, step):
                nc.vector.quantize_mx(
                    out=codes[:, c : c + step].bitcast(E4M3),
                    scales=plane[:, c : c + step],
                    in_=flat[:, PACK * c : PACK * (c + step)],
                )
            wq[key] = (codes, plane)

        def stationary(key, t):
            codes, plane = wq[key]
            cols = slice(t * P, (t + 1) * P)
            return codes[:, cols].bitcast(E4M3), plane[:, cols]

        v0 = keep.tile([P, S], U32, name="v0", align_bytes=64)
        v_plane = keep.tile([P, S], U8, name="v_plane", align_bytes=64)
        v1 = [keep.tile([P, BANK], U32, name="v1_%d" % i, align_bytes=64) for i in range(2)]

        def gather0():
            nc.vector.tensor_copy(v0[:], tab0[:].indirect(offsets[:]))

        def gather_scales():
            nc.vector.tensor_copy(v_plane[:], tab_plane[:].indirect(offsets[:]))

        def gather1(half):
            nc.vector.tensor_copy(
                v1[half][:], tab1[:].indirect(offsets[:, 32 * half : 32 * half + 32])
            )

        h_codes = [keep.tile([P, S], U32, name="h_codes%d" % b, align_bytes=64) for b in range(2)]
        h_plane = [keep.tile([P, S], U8, name="h_plane%d" % b, align_bytes=64) for b in range(2)]
        cap = [keep.tile([P, PACK, BANK], F32, name="cap%d" % i) for i in range(2)]

        def damping(b, j0, n, square_on_vector, by_tokens=False):
            damp = ring.tile([P, PACK, n], F32, name="damp", bufs=4)
            cols = slice(j0, j0 + n)
            per_bank = BANK // n
            for t0 in range(0, PACK, per_bank):
                tex = psum.tile([P, per_bank, n], F32, name="tex", bufs=4)
                for i in range(per_bank):
                    for a in range(2):
                        codes, plane = stationary(("w1", a, b), t0 + i)
                        nc.tensor.matmul_mx(
                            out=tex[:, i, :],
                            lhsT=codes,
                            lhsT_scale=plane,
                            rhs=(v0[:, cols] if a == 0 else v1[j0 // BANK][:, j0 % BANK : j0 % BANK + n]).bitcast(E4M3),
                            rhs_scale=v_plane[4 * a : P, cols],
                            start=(a == 0),
                            stop=(a == 1),
                        )
                for i in range(per_bank):
                    t = t0 + i
                    nc.scalar.activation(damp[:, t, :], tex[:, i, :], ACT.Square, bias=b1_sb[:, b, t : t + 1])
            pairs = [damp[:, 2 * u : 2 * u + 2, :] for u in range(2)]
            if by_tokens:
                pairs = [damp[:, :, u * n // 2 : (u + 1) * n // 2] for u in range(2)]
            for pair in pairs:
                nc.scalar.activation(pair, pair, ACT.Abs_reciprocal_sqrt, bias=1.0)
            squared(pairs, square_on_vector)
            held[b, j0] = pairs
            return damp

        def squared(pairs, square_on_vector):
            for u, pair in enumerate(pairs):
                if square_on_vector[u] == "-":
                    continue
                if square_on_vector[u] == "v":
                    nc.vector.tensor_tensor(pair, pair, pair, ALU.mult)
                elif square_on_vector[u] == "g":
                    for i in range(pair.shape[1]):
                        nc.gpsimd.tensor_tensor(pair[:, i, :], pair[:, i, :], pair[:, i, :], ALU.mult)
                else:
                    nc.scalar.activation(pair, pair, ACT.Square)

        def damped(b, j0, n, damp, off):
            h = ring.tile([P, n, PACK], BF16, name="h", align_bytes=64, bufs=4)
            for c in range(n // CHUNK):
                cols = slice(j0 + c * CHUNK, j0 + (c + 1) * CHUNK)
                wet = psum.tile([P, PACK, CHUNK], F32, name="wet", bufs=2)
                for t in range(PACK):
                    codes, plane = stationary(("w2", 0, b), t)
                    nc.tensor.matmul_mx(
                        out=wet[:, t, :],
                        lhsT=codes,
                        lhsT_scale=plane,
                        rhs=xs[:, cols].bitcast(E4M3),
                        rhs_scale=xs_plane[:, cols],
                        start=True,
                        stop=True,
                    )
                nc.vector.tensor_tensor(
                    h[:, c * CHUNK : (c + 1) * CHUNK, :].rearrange("p (c e) t -> p c t e", e=2),
                    wet[:].rearrange("p t (c e) -> p c t e", e=2),
                    damp[:, :, off + c * CHUNK : off + (c + 1) * CHUNK].rearrange("p t (c e) -> p c t e", e=2),
                    ALU.mult,
                )
            return h

        def quantise_h(b, j0, n, h):
            cols = slice(j0, j0 + n)
            nc.vector.quantize_mx(
                out=h_codes[b][:, cols].bitcast(E4M3), scales=h_plane[b][:, cols], in_=h[:].rearrange("p c t -> p (c t)")
            )

        def scores(j0):
            cols = slice(j0, j0 + CHUNK)
            y = psum.tile([P, PACK, CHUNK], F32, name="y", bufs=2)
            for g in range(PACK):
                for a in range(2):
                    nc.tensor.matmul_mx(
                        out=y[:, g, :],
                        lhsT=w4[:, a, 2 * g * P : 2 * (g + 1) * P].bitcast(E2M1),
                        lhsT_scale=w4_plane[:, a, g * P : (g + 1) * P],
                        rhs=h_codes[a][:, cols].bitcast(E4M3),
                        rhs_scale=h_plane[a][:, cols],
                        start=(a == 0),
                        stop=(a == 1),
                    )
            res = ring.tile([P, PACK, CHUNK], F32, name="res", bufs=4)
            nc.vector.tensor_tensor(res[:], y[:], cap[j0 // BANK][:, :, j0 % BANK : j0 % BANK + CHUNK], ALU.min)
            nc.sync.dma_start(out[:, cols].rearrange("(g p) j -> p g j", p=P), res[:])

        def scores_wide(half, g):
            cols = slice(half * BANK, (half + 1) * BANK)
            y = psum.tile([P, BANK], F32, name="y", bufs=2)
            for a in range(2):
                nc.tensor.matmul_mx(
                    out=y[:],
                    lhsT=w4[:, a, 2 * g * P : 2 * (g + 1) * P].bitcast(E2M1),
                    lhsT_scale=w4_plane[:, a, g * P : (g + 1) * P],
                    rhs=h_codes[a][:, cols].bitcast(E4M3),
                    rhs_scale=h_plane[a][:, cols],
                    start=(a == 0),
                    stop=(a == 1),
                )
            res = ring.tile([P, BANK], F32, name="res", bufs=4)
            nc.vector.tensor_tensor(res[:], y[:], cap[half][:, g, :], ALU.min)
            nc.sync.dma_start(out[g * P : (g + 1) * P, cols], res[:])

        def open_scores(j0):
            cols = slice(j0, j0 + CHUNK)
            banks = []
            for g in range(PACK):
                y = psum.tile([P, CHUNK], F32, name="tex", bufs=4)
                score_pass(y, g, 0, cols)
                banks.append(y)
            return banks

        def score_pass(y, g, a, cols):
            nc.tensor.matmul_mx(
                out=y[:],
                lhsT=w4[:, a, 2 * g * P : 2 * (g + 1) * P].bitcast(E2M1),
                lhsT_scale=w4_plane[:, a, g * P : (g + 1) * P],
                rhs=h_codes[a][:, cols].bitcast(E4M3),
                rhs_scale=h_plane[a][:, cols],
                start=(a == 0),
                stop=(a == 1),
            )

        def close_scores(j0, banks):
            cols = slice(j0, j0 + CHUNK)
            for g in range(PACK):
                score_pass(banks[g], g, 1, cols)
            for u, queue in enumerate((nc.sync, nc.scalar)):
                res = ring.tile([P, 2, CHUNK], F32, name="res", bufs=4)
                for i in range(2):
                    g = 2 * u + i
                    nc.vector.tensor_tensor(
                        res[:, i, :], banks[g][:], cap[j0 // BANK][:, g, j0 % BANK : j0 % BANK + CHUNK], ALU.min
                    )
                queue.dma_start(
                    out[2 * u * P : 2 * (u + 1) * P, cols].rearrange("(g p) j -> p g j", p=P), res[:]
                )

        def caps(half, on_scalar, j0=0, n=BANK):
            cols = slice(half * BANK + j0, half * BANK + j0 + n)
            per_bank = BANK // n
            for g0 in range(0, PACK, per_bank):
                acc = psum.tile([P, per_bank, n], F32, name="tex" if on_scalar[g0] else "y", bufs=4 if on_scalar[g0] else 2)
                for i in range(per_bank):
                    codes, plane = stationary(("w3", 0, 0), g0 + i)
                    nc.tensor.matmul_mx(
                        out=acc[:, i, :],
                        lhsT=codes,
                        lhsT_scale=plane,
                        rhs=xs[:, cols].bitcast(E4M3),
                        rhs_scale=xs_plane[:, cols],
                        start=True,
                        stop=True,
                    )
                for i in range(per_bank):
                    g = g0 + i
                    if on_scalar[g]:
                        nc.scalar.activation(cap[half][:, g, j0 : j0 + n], acc[:, i, :], ACT.Identity, bias=b3_sb[:, g : g + 1])
                    else:
                        nc.vector.tensor_scalar(cap[half][:, g, j0 : j0 + n], acc[:, i, :], b3_sb[:, g : g + 1], None, ALU.add)

        gather0()
        gather_scales()
        quantise(("w1", 0, 0), cast(("w1", 0, 0), "s", 4))
        quantise(("w1", 1, 0), cast(("w1", 1, 0), "s", 4))
        gather1(0)
        d00 = damping(0, 0, 512, "--")
        gather1(1)
        d01 = damping(0, 512, 512, "ss")
        quantise(("w2", 0, 0), cast(("w2", 0, 0), "v", 4), 1)
        quantise(("w1", 0, 1), cast(("w1", 0, 1), "v", 4), 1)
        quantise(("w1", 1, 1), cast(("w1", 1, 1), "v", 4), 1)
        d10 = damping(1, 0, 512, "ss")
        squared(held[0, 0], "vv")
        h = damped(0, 0, 512, d00, 0)
        squared(held[0, 512], "--")
        quantise_h(0, 0, 512, h)
        quantise(("w3", 0, 0), cast(("w3", 0, 0), "v", 4), 1)
        quantise(("w2", 0, 1), cast(("w2", 0, 1), "v", 4), 1)
        hb = damped(0, 512, 512, d01, 0)
        quantise_h(0, 512, 512, hb)
        d12 = damping(1, 512, 256, "ss")
        ha = damped(1, 0, 512, d10, 0)
        caps(0, (1,0,1,0))
        quantise_h(1, 0, 512, ha)
        caps(1, (1,1,1,1), 0, 256)
        d13 = damping(1, 768, 256, "ss", True)
        caps(1, (1,1,1,1), 256, 256)
        scores_wide(0, 0)
        scores_wide(0, 1)
        h = damped(1, 512, 256, d12, 0)
        scores_wide(0, 2)
        quantise_h(1, 512, 256, h)
        scores_wide(0, 3)
        scores(512)
        last = open_scores(896)
        hb = damped(1, 768, 128, d13, 0)
        scores(640)
        quantise_h(1, 768, 128, hb)
        hc = damped(1, 896, 128, d13, 128)
        quantise_h(1, 896, 128, hc)
        scores(768)
        close_scores(896, last)
